import numpy as np
import ml_dtypes


def mxq(x, axis, fmt="e4m3"):
    dtype, down = {"e4m3": (ml_dtypes.float8_e4m3fn, 7), "e5m2": (ml_dtypes.float8_e5m2, 14)}[fmt]
    v = np.moveaxis(np.asarray(x, np.float32).astype(ml_dtypes.bfloat16).astype(np.float64), axis, -1)
    blocks = v.reshape(v.shape[:-1] + (-1, 32))
    amax = np.abs(blocks).max(-1, keepdims=True)
    byte = np.maximum(np.where(amax > 0, np.frexp(amax)[1] - 1 + 127, 0) - down, 1)
    scale = np.exp2(byte - 127.0)
    codes = (blocks / scale).astype(np.float32).astype(dtype).astype(np.float64)
    return np.moveaxis((codes * scale).reshape(v.shape), -1, axis)


WIDE = False


def mx_kscale(k):
    if not WIDE:
        return np.ones(k)
    levels = np.array([10, -10, 5, -5, 0])
    if k % 512:
        return np.exp2(np.random.permutation(np.resize(levels, k // 32))).repeat(32)
    a = np.empty((k // 512, 16))
    for p in range(k // 512):
        a[p, :8] = np.random.permutation(np.resize(levels, 8))
        for g in range(8):
            far = levels[np.abs(levels - a[p, g]) >= 10]
            a[p, g + 8] = far[np.random.randint(len(far))]
    return np.exp2(a.ravel()).repeat(32)


def f64(x):
    return np.asarray(x).astype(np.float64)


def striped(idx):
    return np.tile(idx.reshape(-1, 16).T, (8, 1)).astype(np.uint16)


def unstriped(offs):
    return offs[:16].T.reshape(-1).astype(np.int64)


E2M1 = np.array([0.0, 0.5, 1.0, 1.5, 2.0, 3.0, 4.0, 6.0, -0.0, -0.5, -1.0, -1.5, -2.0, -3.0, -4.0, -6.0])


def pack_weight(w, fmt):
    k, n = w.shape
    w = f64(np.asarray(w, np.float32).astype(ml_dtypes.bfloat16)).reshape(k // 32, 32, n)
    amax = np.abs(w).max(1)
    if fmt == "e4m3":
        byte = np.frexp(amax)[1] - 1 + 127 - 7
    else:
        mant, ex = np.frexp(amax / 6.0)
        byte = np.where(mant > 0.5, ex, ex - 1) + 127
    byte = np.clip(np.where(amax > 0, byte, 1), 1, 254)
    scaled = (w * np.exp2(127.0 - byte)[:, None, :]).reshape(k, n).astype(np.float32)
    by_word = np.ascontiguousarray(scaled.reshape(k // 512, 128, 4, n).transpose(0, 1, 3, 2))
    if fmt == "e4m3":
        words = by_word.astype(ml_dtypes.float8_e4m3fn).view(np.uint8)
    else:
        c = by_word.astype(ml_dtypes.float4_e2m1fn).view(np.uint8) & 0xF
        words = (c[..., 0::2] | (c[..., 1::2] << 4)).reshape(k // 512, 128, 2 * n)
    return np.ascontiguousarray(words), np.ascontiguousarray(byte.astype(np.uint8).reshape(k // 512, 16, n))


def unpack_weight(words, scales, fmt):
    g, _, n = scales.shape
    words = np.ascontiguousarray(words).reshape(g, 128, n, -1)
    if fmt == "e4m3":
        vals = words.view(ml_dtypes.float8_e4m3fn).astype(np.float64)
    else:
        nib = np.empty((g, 128, n, 4), np.uint8)
        nib[..., 0::2] = words & 0xF
        nib[..., 1::2] = words >> 4
        vals = E2M1[nib]
    vals = vals * np.repeat(np.exp2(scales.astype(np.float64) - 127.0), 8, axis=1)[..., None]
    return vals.transpose(0, 1, 3, 2).reshape(g * 512, n)


def gelu(v):
    return 0.5 * v * (1.0 + np.tanh(np.sqrt(2.0 / np.pi) * (v + 0.044715 * v**3)))


K, T, S, K2, T3, P, H, N = 1536, 2048, 1024, 1024, 2048, 512, 512, 640

def setup_inputs():
    n = np.random.standard_normal
    s = mx_kscale(K)[:, None]
    s2 = mx_kscale(K2)[:, None]
    u = mx_kscale(H)[:, None]
    d = {}
    d["tab_words"], d["tab_scales"] = pack_weight(n((K, T)) * s, "e4m3")
    d["offs"] = striped(np.random.permutation(T)[:S])
    d["tab2_words"], d["tab2_scales"] = pack_weight(n((K2, T3)) * s2, "e4m3")
    d["offs2"] = striped(np.random.permutation(T3)[:P])
    d["pos1"] = striped(np.random.permutation(S)[:P])
    d["w1"] = (n((K, H)) / K ** 0.5 / s * u.T).astype(np.float32)
    sign = np.random.choice([-1.0, 1.0], H)
    d["turn"] = (sign * np.random.uniform(0.42, 0.58, H) / u[:, 0]).astype(np.float32)
    d["swing"] = (np.exp(0.3 * n(H)) * u[:, 0]).astype(np.float32)
    d["ws_words"], d["ws_scales"] = pack_weight(3.0 * n((H, H)) / H ** 0.5 / u * u.T, "e2m1")
    d["wb_words"], d["wb_scales"] = pack_weight(1.4 * n((K2, H)) / K2 ** 0.5 / s2, "e4m3")
    d["grip"] = (1.3 * np.exp(0.3 * n(H)) * u[:, 0]).astype(np.float32)
    d["wgs"] = np.exp(0.3 * n((128, P))).astype(np.float32)
    d["wo"] = (n((H, N)) / H ** 0.5 / u).astype(np.float32)
    return d

def reference(tab_words, tab_scales, offs, tab2_words, tab2_scales, offs2, pos1, w1, turn, swing,
              ws_words, ws_scales, wb_words, wb_scales, grip, wgs, wo):
    v = unpack_weight(tab_words, tab_scales, "e4m3")[:, unstriped(offs)]
    v2 = unpack_weight(tab2_words, tab2_scales, "e4m3")[:, unstriped(offs2)]
    c = mxq(f64(w1), 0, "e4m3").T @ v
    x = np.sin(c * f64(turn)[:, None]) * f64(swing)[:, None]
    ws = unpack_weight(ws_words, ws_scales, "e2m1")
    a = np.maximum(c, ws.T @ mxq(x, 0, "e4m3"))
    wb = unpack_weight(wb_words, wb_scales, "e4m3")
    b = np.tanh(wb.T @ v2) * f64(grip)[:, None]
    placed = np.zeros((H, S))
    placed[:, unstriped(pos1)] = np.tile(f64(wgs), (H // 128, 1)) * b
    z = a + placed
    return mxq(f64(wo), 0, "e4m3").T @ mxq(z, 0, "e4m3")

@@ -1,0 +1,311 @@
+import math
+from contextlib import ExitStack
+
+import concourse.mybir as mybir
+from concourse.masks import make_identity
+
+K, T, S, K2, PS, H, N = 1536, 2048, 1024, 1024, 512, 512, 640
+FLOPS = 2 * (K * H * S + H * H * S + K2 * H * PS + H * N * S)
+
+F32 = mybir.dt.float32
+BF16 = mybir.dt.bfloat16
+I32 = mybir.dt.int32
+U32 = mybir.dt.uint32
+U16 = mybir.dt.uint16
+U8 = mybir.dt.uint8
+FP8X4 = mybir.dt.float8_e4m3fn_x4
+FP4X4 = mybir.dt.float4_e2m1fn_x4
+ALU = mybir.AluOpType
+ACT = mybir.ActivationFunctionType
+
+P = 128
+HALF = 512
+TWO_PI = 2.0 * math.pi
+
+
+def tile_list_rockfall_net_scorer_kernel(
+    tc, tab_words, tab_scales, offs, tab2_words, tab2_scales, offs2, pos1, w1, turn, swing,
+    ws_words, ws_scales, wb_words, wb_scales, grip, wgs, wo, out,
+):
+    nc = tc.nc
+    with ExitStack() as ctx:
+        keep = ctx.enter_context(tc.tile_pool(name="keep", bufs=1))
+        ring = ctx.enter_context(tc.tile_pool(name="ring", bufs=2))
+        psum = ctx.enter_context(tc.psum_pool(name="psum", bufs=8))
+
+        idx = keep.tile([P, S // 16], U16, name="idx")
+        idx2 = keep.tile([P, PS // 16], U16, name="idx2")
+        place = keep.tile([P, PS // 16], U16, name="place")
+
+        tab2_sc = keep.tile([P, T], U8, name="tab2_sc", align_bytes=64)
+        tab_sc = keep.tile([P, T], U8, name="tab_sc", align_bytes=64)
+        wbsc_raw = keep.tile([P, H], U8, name="wbsc_raw", align_bytes=64)
+        wssc_raw = keep.tile([P, H], U8, name="wssc_raw", align_bytes=64)
+        nc.vector.memset(tab2_sc[:].bitcast(I32), 0)
+        nc.vector.memset(wbsc_raw[:].bitcast(I32), 0)
+        nc.vector.memset(tab_sc[:].bitcast(I32), 0)
+        nc.vector.memset(wssc_raw[:].bitcast(I32), 0)
+        warm = keep.tile([P, 8], F32, name="warm")
+        warm2 = keep.tile([P, 8], F32, name="warm2")
+        nc.gpsimd.memset(warm[:], 0.0)
+        nc.scalar.activation(out=warm2[:], in_=warm[:], func=ACT.Silu)
+        placed = [None] * 4
+        placed[0] = keep.tile([P, S], F32, name="placed0", align_bytes=64)
+        nc.vector.memset(placed[0][:], 0.0)
+        placed[1] = keep.tile([P, S], F32, name="placed1", align_bytes=64)
+        nc.vector.memset(placed[1][:], 0.0)
+        placed[2] = keep.tile([P, S], F32, name="placed2", align_bytes=64)
+        nc.vector.memset(placed[2][:], 0.0)
+        placed[3] = keep.tile([P, S], F32, name="placed3", align_bytes=64)
+        nc.vector.memset(placed[3][:], 0.0)
+
+        def words_view(words, a):
+            return words[a].rearrange("p t i -> p (t i)").bitcast(I32)
+
+        tab2_win = [keep.tile([P, T], U32, name="tab2_win0", align_bytes=64), keep.tile([P, T], U32, name="tab2_win1", align_bytes=64)]
+        tab_win = [keep.tile([P, T], U32, name="tab_win0", tag="H", align_bytes=64), keep.tile([P, T], U32, name="tab_win1", tag="I", align_bytes=64), keep.tile([P, T], U32, name="tab_win2", align_bytes=64)]
+        w1_raw = [keep.tile([P, 4, H], F32, name="w1_raw0", tag="C", align_bytes=64), keep.tile([P, 4, H], F32, name="w1_raw1", align_bytes=64), keep.tile([P, 4, H], F32, name="w1_raw2", align_bytes=64)]
+        wb_raw = keep.tile([P, 2, H], U32, name="wb_raw", align_bytes=64)
+        ws_raw = keep.tile([P, 2 * H], U8, name="ws_raw", align_bytes=64)
+        wo_raw = keep.tile([P, 4, N], F32, name="wo_raw", tag="C", align_bytes=64)
+        wg = keep.tile([P, 4, PS], F32, name="wg")
+        wgs_sb = keep.tile([P, PS], F32, name="wgs_sb")
+        turn_sb = keep.tile([P, 4], F32, name="turn_sb")
+        swing_sb = keep.tile([P, 4], F32, name="swing_sb")
+        grip_sb = keep.tile([P, 4], F32, name="grip_sb")
+        w1_rows = w1.rearrange("(a p j) c -> a p j c", a=3, j=4)
+
+        def load_scale_rows(queue, plane, scales):
+            rows = 4 * scales.shape[0]
+            for q in range(4):
+                queue.dma_start(plane[32 * q : 32 * q + rows, :].bitcast(I32), scales[:, 4 * q : 4 * q + 4, :].bitcast(I32))
+
+
+        nc.sync.dma_start(idx[:], offs)
+        nc.sync.dma_start(tab_win[0][:].bitcast(I32), words_view(tab_words, 0))
+        load_scale_rows(nc.scalar, tab_sc, tab_scales)
+        nc.sync.dma_start(wgs_sb[:], wgs)
+        nc.scalar.dma_start(grip_sb[:], grip.rearrange("(p t) -> p t", t=4))
+        nc.scalar.dma_start(turn_sb[:], turn.rearrange("(p t) -> p t", t=4))
+        nc.scalar.dma_start(swing_sb[:], swing.rearrange("(p t) -> p t", t=4))
+        nc.sync.dma_start(w1_raw[0][:], w1_rows[0])
+        nc.sync.dma_start(tab_win[1][:].bitcast(I32), words_view(tab_words, 1))
+        nc.sync.dma_start(idx2[:], offs2)
+        load_scale_rows(nc.sync, tab2_sc, tab2_scales)
+        nc.sync.dma_start(w1_raw[1][:], w1_rows[1])
+        nc.sync.dma_start(wb_raw[:].bitcast(I32), wb_words.rearrange("a p e i -> p a (e i)").bitcast(I32))
+        load_scale_rows(nc.sync, wbsc_raw, wb_scales)
+        nc.sync.dma_start(w1_raw[2][:], w1_rows[2])
+        nc.sync.dma_start(ws_raw[:].bitcast(I32), ws_words[0].bitcast(I32))
+        load_scale_rows(nc.sync, wssc_raw, ws_scales)
+        nc.sync.dma_start(tab_win[2][:].bitcast(I32), words_view(tab_words, 2))
+        nc.sync.dma_start(tab2_win[0][:].bitcast(I32), words_view(tab2_words, 0))
+        nc.sync.dma_start(tab2_win[1][:].bitcast(I32), words_view(tab2_words, 1))
+        nc.sync.dma_start(place[:], pos1)
+        nc.sync.dma_start(wo_raw[:], wo.rearrange("(p j) n -> p j n", j=4))
+
+        ident = keep.tile([P, P], F32, name="ident")
+        make_identity(nc, ident[:])
+        turned = psum.tile([P, 4, P], F32, name="bank")
+        for b in range(4):
+            nc.tensor.transpose(turned[:, b, :], wgs_sb[:, P * b : P * (b + 1)], ident[:])
+        spread = []
+        dealt = keep.tile([P, 4, 4, P], F32, name="dealt", tag="F", align_bytes=64)
+        for t in range(4):
+            nc.scalar.copy(
+                dealt[:, t, :, :].rearrange("p b (r q) -> p b r q", r=4),
+                turned[:].rearrange("p b (q t) -> p b t q", t=4)[:, :, t : t + 1, :].to_broadcast([P, 4, 4, 32]),
+            )
+            bank = psum.tile([P, 4, P], F32, name="bank")
+            for b in range(4):
+                nc.tensor.transpose(bank[:, b, :], dealt[:, t, b, :], ident[:])
+            spread.append(bank)
+
+        v2_sc = keep.tile([P, PS], U8, name="v2_sc", align_bytes=64)
+        v_sc = keep.tile([P, S], U8, name="v_sc", align_bytes=64)
+        v2 = [keep.tile([P, PS], U32, name=f"survey{a}", align_bytes=64) for a in range(2)]
+        for a in range(2):
+            nc.vector.tensor_copy(v2[a][:], tab2_win[a][:].indirect(idx2[:]))
+        nc.vector.tensor_copy(v2_sc[:], tab2_sc[:].indirect(idx2[:]))
+
+        wb_q = keep.tile([P, 2, H], U32, name="wb_q", align_bytes=64)
+        wb_sc = keep.tile([P, H], U8, name="wb_sc", align_bytes=64)
+        nc.vector.tensor_copy(
+            wb_q[:].bitcast(I32).rearrange("p a (t q) -> p a q t", t=4),
+            wb_raw[:].bitcast(I32).rearrange("p a (q t) -> p a q t", t=4),
+        )
+        nc.vector.tensor_copy(wb_sc[:].rearrange("p (t q) -> p q t", t=4), wbsc_raw[:].rearrange("p (q t) -> p q t", t=4))
+        def scatter(t, factor):
+            for u in range(1):
+                n = PS // 1
+                nc.vector.tensor_tensor(
+                    placed[t][:].indirect(place[:, n // 16 * u : n // 16 * (u + 1)]),
+                    th[t][:, n * u : n * (u + 1)], factor[:, n * u : n * (u + 1)], ALU.mult,
+                )
+
+
+        v = [[keep.tile([P, HALF], U32, name=f"v{a}_{h}", align_bytes=64) for h in range(2)] for a in range(3)]
+        w1_q = [keep.tile([P, H], U32, name=f"w1_q{a}", align_bytes=64) for a in range(3)]
+        w1_sc = [keep.tile([P, H], U8, name=f"w1_sc{a}", align_bytes=64) for a in range(3)]
+        nc.vector.tensor_copy(v_sc[:], tab_sc[:].indirect(idx[:]))
+        w1_bfs = [keep.tile([P, 4 * H], BF16, name=f"w1_bf{a}", align_bytes=64) for a in range(3)]
+        for a in range(3):
+            w1_bf = w1_bfs[a]
+            nc.scalar.copy(
+                w1_bf[:].rearrange("p (t m j) -> p m j t", t=4, j=4),
+                w1_raw[a][:].rearrange("p j (m t) -> p m j t", t=4),
+            )
+            nc.vector.quantize_mx(out=w1_q[a][:].bitcast(FP8X4), scales=w1_sc[a][:], in_=w1_bf[:])
+            for h in range(2):
+                nc.vector.tensor_copy(v[a][h][:], tab_win[a][:].indirect(idx[:, 32 * h : 32 * (h + 1)]))
+
+        for t in range(4):
+            nc.scalar.activation(
+                out=wg[:, t, :], in_=spread[t][:].rearrange("p b j -> p (b j)"), func=ACT.Copy, scale=grip_sb[:, t : t + 1]
+            )
+        turns = keep.tile([P, 4], F32, name="turns")
+        nc.vector.tensor_scalar(turns[:], turn_sb[:], 1.0 / TWO_PI, 0.0, ALU.mult, ALU.add)
+
+        c_sb = [keep.tile([P, 4, HALF], F32, name="c_sb0", align_bytes=64), keep.tile([P, 4, HALF], F32, name="c_sb1", tag="H", align_bytes=64)]
+        x_q = [keep.tile([P, HALF], U32, name=f"x_q{h}", align_bytes=64) for h in range(2)]
+        x_sc = [keep.tile([P, HALF], U8, name=f"x_sc{h}", align_bytes=64) for h in range(2)]
+
+        wholes = [keep.tile([P, HALF], I32, name=f"whole{i}") for i in range(4)]
+        x_bfs = [keep.tile([P, 4 * HALF], BF16, name=f"x_bf{h}", align_bytes=64) for h in range(2)]
+
+        fracs = [keep.tile([P, 4, HALF], F32, name="frac0", tag="F", align_bytes=64), keep.tile([P, 4, HALF], F32, name="frac1", tag="I", align_bytes=64)]
+
+        late = keep.tile([P, 4 * S], F32, name="late", align_bytes=64)
+        joined = late[:, 0 : 4 * S].rearrange("p (t j) -> p t j", t=4)
+        wo_bf = keep.tile([P, 4 * N], BF16, name="wo_bf", align_bytes=64)
+        x_room0 = keep.tile([P, 2 * HALF], F32, name="x_room0", align_bytes=64)
+        x_rooms = [x_room0[:].bitcast(BF16), late[:, 3 * S : 4 * S].bitcast(BF16)]
+
+        def load_features(h):
+            frac = fracs[h]
+            for t in range(4):
+                cols = slice(P * t, P * (t + 1))
+                bank = psum.tile([P, HALF], F32, name="bank")
+                for a in range(3):
+                    nc.tensor.matmul_mx(
+                        out=bank[:], lhsT=w1_q[a][:, cols].bitcast(FP8X4), lhsT_scale=w1_sc[a][:, cols],
+                        rhs=v[a][h][:].bitcast(FP8X4), rhs_scale=v_sc[4 * a : P, HALF * h : HALF * (h + 1)],
+                        start=(a == 0), stop=(a == 2),
+                    )
+                nc.scalar.copy(c_sb[h][:, t, :], bank[:])
+                whole = wholes[(4 * h + t) % len(wholes)]
+                nc.vector.tensor_scalar(whole[:], c_sb[h][:, t, :], turns[:, t : t + 1], 1.0, ALU.mult, ALU.add)
+                nc.vector.scalar_tensor_tensor(
+                    frac[:, t, :], c_sb[h][:, t, :], turns[:, t : t + 1], whole[:], ALU.mult, ALU.subtract
+                )
+
+        def swing_features(h, on_vector):
+            frac = fracs[h]
+            x_bf = x_bfs[h]
+            x_rows = x_rooms[h].rearrange("p (t j) -> p t j", t=4)
+            for t in range(4):
+                nc.scalar.activation(out=frac[:, t, :], in_=frac[:, t, :], func=ACT.Sin, scale=TWO_PI, bias=TWO_PI)
+                if not on_vector:
+                    nc.scalar.activation(out=x_rows[:, t, :], in_=frac[:, t, :], func=ACT.Copy, scale=swing_sb[:, t : t + 1])
+            woven = x_bf[:].rearrange("p (c i t) -> p c t i", i=4, t=4)
+            if on_vector:
+                nc.vector.tensor_tensor(
+                    woven, frac[:].rearrange("p t (c i) -> p c t i", i=4),
+                    swing_sb[:].unsqueeze(1).unsqueeze(3).to_broadcast([P, HALF // 4, 4, 4]), ALU.mult,
+                )
+            else:
+                nc.scalar.copy(woven, x_rows[:].rearrange("p t (c i) -> p c t i", i=4))
+            nc.vector.quantize_mx(out=x_q[h][:].bitcast(FP8X4), scales=x_sc[h][:], in_=x_bf[:])
+
+        load_features(0)
+        load_features(1)
+        survey = []
+        th = [keep.tile([P, HALF], F32, name="th0"), keep.tile([P, HALF], F32, name="th1"), x_room0[:, 0:HALF], fracs[1][:, 2, :]]
+        for t in range(4):
+            cols = slice(P * t, P * (t + 1))
+            bank = psum.tile([P, HALF], F32, name="bank")
+            for a in range(2):
+                nc.tensor.matmul_mx(
+                    out=bank[:], lhsT=wb_q[:, a, cols].bitcast(FP8X4), lhsT_scale=wb_sc[4 * a : P, cols],
+                    rhs=v2[a][:].bitcast(FP8X4), rhs_scale=v2_sc[4 * a : P, :], start=(a == 0), stop=(a == 1),
+                )
+            survey.append(bank)
+        for t in range(2):
+            nc.scalar.activation(out=th[t][:], in_=survey[t][:], func=ACT.Tanh)
+
+        swing_features(0, False)
+        nc.scalar.activation(out=th[2][:], in_=survey[2][:], func=ACT.Tanh)
+        ws_q = keep.tile([P, 2 * H], U8, name="ws_q", align_bytes=64)
+        ws_sc = keep.tile([P, H], U8, name="ws_sc", align_bytes=64)
+        nc.vector.tensor_copy(
+            ws_q[:].rearrange("p (t q b) -> p q t b", t=4, b=2), ws_raw[:].rearrange("p (q t b) -> p q t b", t=4, b=2)
+        )
+        nc.vector.tensor_copy(ws_sc[:].rearrange("p (t q) -> p q t", t=4), wssc_raw[:].rearrange("p (q t) -> p q t", t=4))
+        swing_features(1, False)
+
+
+        nc.scalar.activation(out=th[3][:], in_=survey[3][:], func=ACT.Tanh)
+        wo_q = keep.tile([P, N], U32, name="wo_q", align_bytes=64)
+        wo_sc = keep.tile([P, N], U8, name="wo_sc", align_bytes=64)
+        nc.scalar.copy(
+            wo_bf[:].rearrange("p (c i j) -> p c j i", i=4, j=4), wo_raw[:].rearrange("p j (c i) -> p c j i", i=4)
+        )
+        for lo, hi in ((0, 512), (512, N)):
+            nc.vector.quantize_mx(out=wo_q[:, lo:hi].bitcast(FP8X4), scales=wo_sc[:, lo:hi], in_=wo_bf[:, 4 * lo : 4 * hi])
+
+        for t in range(4):
+            scatter(t, wg[:, t, :])
+        for t in range(3):
+            nc.sync.dma_start(joined[:, t, :], placed[t][:])
+        for h in range(2):
+            nc.scalar.copy(joined[:, 3, HALF * h : HALF * (h + 1)], placed[3][:, HALF * h : HALF * (h + 1)])
+        flat = "p a b -> p (a b)"
+        rooms = [w1_raw[1][:].rearrange(flat), w1_raw[2][:].rearrange(flat), wo_raw[:].rearrange(flat)]
+        stages = [rooms[0], rooms[1]] + [rooms[2][:, 640 * i : 2560] for i in range(4)]
+        swung = [[], []]
+        for h in range(2):
+            for u in range(4):
+                bank = psum.tile([P, 4, P], F32, name="bank")
+                for t in range(4):
+                    nc.tensor.matmul_mx(
+                        out=bank[:, t, :], lhsT=ws_q[:, 2 * P * t : 2 * P * (t + 1)].bitcast(FP4X4), lhsT_scale=ws_sc[:, P * t : P * (t + 1)],
+                        rhs=x_q[h][:, P * u : P * (u + 1)].bitcast(FP8X4), rhs_scale=x_sc[h][:, P * u : P * (u + 1)], start=True, stop=True,
+                    )
+                swung[h].append(bank)
+        out_rows = out.rearrange("(n p) j -> p n j", p=P)
+        for h, pieces in enumerate(((256, 256,), (128, 128, 128, 128,))):
+            larger = fracs[h]
+            z_bf = w1_bfs[h]
+            z_q = ring.tile([P, HALF], U32, name="z_q", align_bytes=64)
+            z_sc = ring.tile([P, HALF], U8, name="z_sc", align_bytes=64)
+            lo = 0
+            for width in pieces:
+                js = slice(lo, lo + width)
+                for u in range(lo // P, (lo + width) // P):
+                    us = slice(P * u, P * (u + 1))
+                    nc.vector.tensor_tensor(larger[:, :, us], swung[h][u][:], c_sb[h][:, :, us], ALU.max)
+                z_piece = z_bf[:, 4 * lo : 4 * (lo + width)]
+                nc.vector.tensor_tensor(
+                    z_piece.rearrange("p (c i t) -> p c t i", i=4, t=4),
+                    larger[:, :, js].rearrange("p t (c i) -> p c t i", i=4),
+                    joined[:, :, HALF * h + lo : HALF * h + lo + width].rearrange("p t (c i) -> p c t i", i=4),
+                    ALU.add,
+                )
+                nc.vector.quantize_mx(out=z_q[:, js].bitcast(FP8X4), scales=z_sc[:, js], in_=z_piece)
+                stage = stages.pop(0)[:, 0 : 5 * width].rearrange("p (n j) -> p n j", n=5)
+                per_bank = HALF // width
+                for b, n0 in enumerate(range(0, 5, per_bank)):
+                    ns = list(range(n0, min(n0 + per_bank, 5)))
+                    bank = psum.tile([P, HALF], F32, name="bank")
+                    for i, n in enumerate(ns):
+                        cols = slice(P * n, P * (n + 1))
+                        nc.tensor.matmul_mx(
+                            out=bank[:, width * i : width * (i + 1)], lhsT=wo_q[:, cols].bitcast(FP8X4), lhsT_scale=wo_sc[:, cols],
+                            rhs=z_q[:, js].bitcast(FP8X4), rhs_scale=z_sc[:, js], start=True, stop=True,
+                        )
+                    last = h == 1 and lo + width == HALF
+                    copy = nc.vector.tensor_copy if last and b == 0 else nc.scalar.copy
+                    copy(stage[:, n0 : n0 + len(ns), :].rearrange("p n j -> p (n j)"), bank[:, 0 : width * len(ns)])
+                j0 = HALF * h + lo
+                nc.sync.dma_start(out_rows[:, :, j0 : j0 + width], stage[:])
+                lo += width

@@ -135,6 +135,7 @@ def tile_list_rockfall_net_scorer_kernel(
             wb_raw[:].bitcast(I32).rearrange("p a (q t) -> p a q t", t=4),
         )
         nc.vector.tensor_copy(wb_sc[:].rearrange("p (t q) -> p q t", t=4), wbsc_raw[:].rearrange("p (q t) -> p q t", t=4))
+
         def scatter(t, factor):
             for u in range(1):
                 n = PS // 1
@@ -175,7 +176,7 @@ def tile_list_rockfall_net_scorer_kernel(
 
         fracs = [keep.tile([P, 4, HALF], F32, name="frac0", tag="F", align_bytes=64), keep.tile([P, 4, HALF], F32, name="frac1", tag="I", align_bytes=64)]
 
-        late = keep.tile([P, 4 * S], F32, name="late", align_bytes=64)
+        late = keep.tile([P, 4 * S + 0], F32, name="late", align_bytes=64)
         joined = late[:, 0 : 4 * S].rearrange("p (t j) -> p t j", t=4)
         wo_bf = keep.tile([P, 4 * N], BF16, name="wo_bf", align_bytes=64)
         x_room0 = keep.tile([P, 2 * HALF], F32, name="x_room0", align_bytes=64)
@@ -194,9 +195,9 @@ def tile_list_rockfall_net_scorer_kernel(
                     )
                 nc.scalar.copy(c_sb[h][:, t, :], bank[:])
                 whole = wholes[(4 * h + t) % len(wholes)]
-                nc.vector.tensor_scalar(whole[:], c_sb[h][:, t, :], turns[:, t : t + 1], 1.0, ALU.mult, ALU.add)
+                nc.gpsimd.tensor_scalar(whole[:], c_sb[h][:, t, :], turns[:, t : t + 1], 1.0, ALU.mult, ALU.add)
                 nc.vector.scalar_tensor_tensor(
-                    frac[:, t, :], c_sb[h][:, t, :], turns[:, t : t + 1], whole[:], ALU.mult, ALU.subtract
+                    frac[:, t, :], bank[:], turns[:, t : t + 1], whole[:], ALU.mult, ALU.subtract
                 )
 
         def swing_features(h, on_vector):
@@ -220,7 +221,7 @@ def tile_list_rockfall_net_scorer_kernel(
         load_features(0)
         load_features(1)
         survey = []
-        th = [keep.tile([P, HALF], F32, name="th0"), keep.tile([P, HALF], F32, name="th1"), x_room0[:, 0:HALF], fracs[1][:, 2, :]]
+        th = [None] * 4
         for t in range(4):
             cols = slice(P * t, P * (t + 1))
             bank = psum.tile([P, HALF], F32, name="bank")
@@ -230,10 +231,13 @@ def tile_list_rockfall_net_scorer_kernel(
                     rhs=v2[a][:].bitcast(FP8X4), rhs_scale=v2_sc[4 * a : P, :], start=(a == 0), stop=(a == 1),
                 )
             survey.append(bank)
-        for t in range(2):
-            nc.scalar.activation(out=th[t][:], in_=survey[t][:], func=ACT.Tanh)
+        th[0] = keep.tile([P, HALF], F32, name="th0")
+        nc.scalar.activation(out=th[0][:], in_=survey[0][:], func=ACT.Tanh)
+        th[1] = keep.tile([P, HALF], F32, name="th1")
+        nc.scalar.activation(out=th[1][:], in_=survey[1][:], func=ACT.Tanh)
 
         swing_features(0, False)
+        th[2] = x_room0[:, 0:HALF]
         nc.scalar.activation(out=th[2][:], in_=survey[2][:], func=ACT.Tanh)
         ws_q = keep.tile([P, 2 * H], U8, name="ws_q", align_bytes=64)
         ws_sc = keep.tile([P, H], U8, name="ws_sc", align_bytes=64)
@@ -244,6 +248,7 @@ def tile_list_rockfall_net_scorer_kernel(
         swing_features(1, False)
 
 
+        th[3] = fracs[1][:, 2, :]
         nc.scalar.activation(out=th[3][:], in_=survey[3][:], func=ACT.Tanh)
         wo_q = keep.tile([P, N], U32, name="wo_q", align_bytes=64)
         wo_sc = keep.tile([P, N], U8, name="wo_sc", align_bytes=64)

@@ -41,14 +41,16 @@ def tile_list_rockfall_net_scorer_kernel(
         tab_sc = keep.tile([P, T], U8, name="tab_sc", align_bytes=64)
         wbsc_raw = keep.tile([P, H], U8, name="wbsc_raw", align_bytes=64)
         wssc_raw = keep.tile([P, H], U8, name="wssc_raw", align_bytes=64)
+        nc.vector.memset(tab_sc[:].bitcast(I32), 0)
         nc.vector.memset(tab2_sc[:].bitcast(I32), 0)
         nc.vector.memset(wbsc_raw[:].bitcast(I32), 0)
-        nc.vector.memset(tab_sc[:].bitcast(I32), 0)
         nc.vector.memset(wssc_raw[:].bitcast(I32), 0)
         warm = keep.tile([P, 8], F32, name="warm")
         warm2 = keep.tile([P, 8], F32, name="warm2")
         nc.gpsimd.memset(warm[:], 0.0)
         nc.scalar.activation(out=warm2[:], in_=warm[:], func=ACT.Silu)
+        ident = keep.tile([P, P], F32, name="ident")
+        make_identity(nc, ident[:])
         placed = [None] * 4
         placed[0] = keep.tile([P, S], F32, name="placed0", align_bytes=64)
         nc.vector.memset(placed[0][:], 0.0)
@@ -88,24 +90,22 @@ def tile_list_rockfall_net_scorer_kernel(
         nc.scalar.dma_start(grip_sb[:], grip.rearrange("(p t) -> p t", t=4))
         nc.scalar.dma_start(turn_sb[:], turn.rearrange("(p t) -> p t", t=4))
         nc.scalar.dma_start(swing_sb[:], swing.rearrange("(p t) -> p t", t=4))
+        load_scale_rows(nc.gpsimd, tab2_sc, tab2_scales)
+        load_scale_rows(nc.gpsimd, wbsc_raw, wb_scales)
         nc.sync.dma_start(w1_raw[0][:], w1_rows[0])
-        nc.sync.dma_start(tab_win[1][:].bitcast(I32), words_view(tab_words, 1))
         nc.sync.dma_start(idx2[:], offs2)
-        load_scale_rows(nc.sync, tab2_sc, tab2_scales)
+        nc.sync.dma_start(tab_win[1][:].bitcast(I32), words_view(tab_words, 1))
         nc.sync.dma_start(w1_raw[1][:], w1_rows[1])
-        nc.sync.dma_start(wb_raw[:].bitcast(I32), wb_words.rearrange("a p e i -> p a (e i)").bitcast(I32))
-        load_scale_rows(nc.sync, wbsc_raw, wb_scales)
-        nc.sync.dma_start(w1_raw[2][:], w1_rows[2])
         nc.sync.dma_start(ws_raw[:].bitcast(I32), ws_words[0].bitcast(I32))
         load_scale_rows(nc.sync, wssc_raw, ws_scales)
+        nc.sync.dma_start(w1_raw[2][:], w1_rows[2])
         nc.sync.dma_start(tab_win[2][:].bitcast(I32), words_view(tab_words, 2))
         nc.sync.dma_start(tab2_win[0][:].bitcast(I32), words_view(tab2_words, 0))
+        nc.sync.dma_start(wb_raw[:].bitcast(I32), wb_words.rearrange("a p e i -> p a (e i)").bitcast(I32))
         nc.sync.dma_start(tab2_win[1][:].bitcast(I32), words_view(tab2_words, 1))
         nc.sync.dma_start(place[:], pos1)
         nc.sync.dma_start(wo_raw[:], wo.rearrange("(p j) n -> p j n", j=4))
 
-        ident = keep.tile([P, P], F32, name="ident")
-        make_identity(nc, ident[:])
         turned = psum.tile([P, 4, P], F32, name="bank")
         for b in range(4):
             nc.tensor.transpose(turned[:, b, :], wgs_sb[:, P * b : P * (b + 1)], ident[:])
@@ -134,7 +134,7 @@ def tile_list_rockfall_net_scorer_kernel(
             wb_q[:].bitcast(I32).rearrange("p a (t q) -> p a q t", t=4),
             wb_raw[:].bitcast(I32).rearrange("p a (q t) -> p a q t", t=4),
         )
-        nc.vector.tensor_copy(wb_sc[:].rearrange("p (t q) -> p q t", t=4), wbsc_raw[:].rearrange("p (q t) -> p q t", t=4))
+        nc.gpsimd.tensor_copy(wb_sc[:].rearrange("p (t q) -> p q t", t=4), wbsc_raw[:].rearrange("p (q t) -> p q t", t=4))
 
         def scatter(t, factor):
             for u in range(1):
@@ -178,9 +178,9 @@ def tile_list_rockfall_net_scorer_kernel(
 
         late = keep.tile([P, 4 * S + 0], F32, name="late", align_bytes=64)
         joined = late[:, 0 : 4 * S].rearrange("p (t j) -> p t j", t=4)
-        wo_bf = keep.tile([P, 4 * N], BF16, name="wo_bf", align_bytes=64)
-        x_room0 = keep.tile([P, 2 * HALF], F32, name="x_room0", align_bytes=64)
-        x_rooms = [x_room0[:].bitcast(BF16), late[:, 3 * S : 4 * S].bitcast(BF16)]
+        x_room0 = keep.tile([P, HALF + 2 * N], F32, name="x_room0", align_bytes=64)
+        wo_bf = x_room0[:, HALF : HALF + 2 * N].bitcast(BF16)
+        x_rooms = [x_room0[:, 0 : 2 * HALF].bitcast(BF16), late[:, 3 * S : 4 * S].bitcast(BF16)]
 
         def load_features(h):
             frac = fracs[h]
@@ -195,7 +195,7 @@ def tile_list_rockfall_net_scorer_kernel(
                     )
                 nc.scalar.copy(c_sb[h][:, t, :], bank[:])
                 whole = wholes[(4 * h + t) % len(wholes)]
-                nc.gpsimd.tensor_scalar(whole[:], c_sb[h][:, t, :], turns[:, t : t + 1], 1.0, ALU.mult, ALU.add)
+                nc.gpsimd.tensor_scalar(whole[:], c_sb[h][:, t, :], turns[:, t : t + 1], 0.0, ALU.mult, ALU.add)
                 nc.vector.scalar_tensor_tensor(
                     frac[:, t, :], bank[:], turns[:, t : t + 1], whole[:], ALU.mult, ALU.subtract
                 )
@@ -205,7 +205,7 @@ def tile_list_rockfall_net_scorer_kernel(
             x_bf = x_bfs[h]
             x_rows = x_rooms[h].rearrange("p (t j) -> p t j", t=4)
             for t in range(4):
-                nc.scalar.activation(out=frac[:, t, :], in_=frac[:, t, :], func=ACT.Sin, scale=TWO_PI, bias=TWO_PI)
+                nc.scalar.activation(out=frac[:, t, :], in_=frac[:, t, :], func=ACT.Sin, scale=TWO_PI)
                 if not on_vector:
                     nc.scalar.activation(out=x_rows[:, t, :], in_=frac[:, t, :], func=ACT.Copy, scale=swing_sb[:, t : t + 1])
             woven = x_bf[:].rearrange("p (c i t) -> p c t i", i=4, t=4)
@@ -245,11 +245,6 @@ def tile_list_rockfall_net_scorer_kernel(
             ws_q[:].rearrange("p (t q b) -> p q t b", t=4, b=2), ws_raw[:].rearrange("p (q t b) -> p q t b", t=4, b=2)
         )
         nc.vector.tensor_copy(ws_sc[:].rearrange("p (t q) -> p q t", t=4), wssc_raw[:].rearrange("p (q t) -> p q t", t=4))
-        swing_features(1, False)
-
-
-        th[3] = fracs[1][:, 2, :]
-        nc.scalar.activation(out=th[3][:], in_=survey[3][:], func=ACT.Tanh)
         wo_q = keep.tile([P, N], U32, name="wo_q", align_bytes=64)
         wo_sc = keep.tile([P, N], U8, name="wo_sc", align_bytes=64)
         nc.scalar.copy(
@@ -258,6 +253,11 @@ def tile_list_rockfall_net_scorer_kernel(
         for lo, hi in ((0, 512), (512, N)):
             nc.vector.quantize_mx(out=wo_q[:, lo:hi].bitcast(FP8X4), scales=wo_sc[:, lo:hi], in_=wo_bf[:, 4 * lo : 4 * hi])
 
+        swing_features(1, False)
+
+
+        th[3] = fracs[1][:, 1, :]
+        nc.scalar.activation(out=th[3][:], in_=survey[3][:], func=ACT.Tanh)
         for t in range(4):
             scatter(t, wg[:, t, :])
         for t in range(3):
@@ -266,7 +266,7 @@ def tile_list_rockfall_net_scorer_kernel(
             nc.scalar.copy(joined[:, 3, HALF * h : HALF * (h + 1)], placed[3][:, HALF * h : HALF * (h + 1)])
         flat = "p a b -> p (a b)"
         rooms = [w1_raw[1][:].rearrange(flat), w1_raw[2][:].rearrange(flat), wo_raw[:].rearrange(flat)]
-        stages = [rooms[0], rooms[1]] + [rooms[2][:, 640 * i : 2560] for i in range(4)]
+        stages = [rooms[0], rooms[0][:, 640:2048], rooms[1]] + [rooms[2][:, 640 * i : 2560] for i in range(4)]
         swung = [[], []]
         for h in range(2):
             for u in range(4):
@@ -278,7 +278,7 @@ def tile_list_rockfall_net_scorer_kernel(
                     )
                 swung[h].append(bank)
         out_rows = out.rearrange("(n p) j -> p n j", p=P)
-        for h, pieces in enumerate(((256, 256,), (128, 128, 128, 128,))):
+        for h, pieces in enumerate(((128, 128, 256,), (128, 128, 128, 128,))):
             larger = fracs[h]
             z_bf = w1_bfs[h]
             z_q = ring.tile([P, HALF], U32, name="z_q", align_bytes=64)

import math
from contextlib import ExitStack

import concourse.mybir as mybir
from concourse.masks import make_identity

K, T, S, K2, PS, H, N = 1536, 2048, 1024, 1024, 512, 512, 640
FLOPS = 2 * (K * H * S + H * H * S + K2 * H * PS + H * N * S)

F32 = mybir.dt.float32
BF16 = mybir.dt.bfloat16
I32 = mybir.dt.int32
U32 = mybir.dt.uint32
U16 = mybir.dt.uint16
U8 = mybir.dt.uint8
FP8X4 = mybir.dt.float8_e4m3fn_x4
FP4X4 = mybir.dt.float4_e2m1fn_x4
ALU = mybir.AluOpType
ACT = mybir.ActivationFunctionType

P = 128
HALF = 512
TWO_PI = 2.0 * math.pi


def tile_list_rockfall_net_scorer_kernel(
    tc, tab_words, tab_scales, offs, tab2_words, tab2_scales, offs2, pos1, w1, turn, swing,
    ws_words, ws_scales, wb_words, wb_scales, grip, wgs, wo, out,
):
    nc = tc.nc
    with ExitStack() as ctx:
        keep = ctx.enter_context(tc.tile_pool(name="keep", bufs=1))
        ring = ctx.enter_context(tc.tile_pool(name="ring", bufs=2))
        psum = ctx.enter_context(tc.psum_pool(name="psum", bufs=8))

        idx = keep.tile([P, S // 16], U16, name="idx")
        idx2 = keep.tile([P, PS // 16], U16, name="idx2")
        place = keep.tile([P, PS // 16], U16, name="place")

        tab2_sc = keep.tile([P, T], U8, name="tab2_sc", align_bytes=64)
        tab_sc = keep.tile([P, T], U8, name="tab_sc", align_bytes=64)
        wbsc_raw = keep.tile([P, H], U8, name="wbsc_raw", align_bytes=64)
        wssc_raw = keep.tile([P, H], U8, name="wssc_raw", align_bytes=64)
        nc.vector.memset(tab_sc[:].bitcast(I32), 0)
        nc.vector.memset(tab2_sc[:].bitcast(I32), 0)
        nc.vector.memset(wbsc_raw[:].bitcast(I32), 0)
        nc.vector.memset(wssc_raw[:].bitcast(I32), 0)
        warm = keep.tile([P, 8], F32, name="warm")
        warm2 = keep.tile([P, 8], F32, name="warm2")
        nc.gpsimd.memset(warm[:], 0.0)
        nc.scalar.activation(out=warm2[:], in_=warm[:], func=ACT.Silu)
        ident = keep.tile([P, P], F32, name="ident")
        make_identity(nc, ident[:])
        placed = [None] * 4
        placed[0] = keep.tile([P, S], F32, name="placed0", align_bytes=64)
        nc.vector.memset(placed[0][:], 0.0)
        placed[1] = keep.tile([P, S], F32, name="placed1", align_bytes=64)
        nc.vector.memset(placed[1][:], 0.0)
        placed[2] = keep.tile([P, S], F32, name="placed2", align_bytes=64)
        nc.vector.memset(placed[2][:], 0.0)
        placed[3] = keep.tile([P, S], F32, name="placed3", align_bytes=64)
        nc.vector.memset(placed[3][:], 0.0)

        def words_view(words, a):
            return words[a].rearrange("p t i -> p (t i)").bitcast(I32)

        tab2_win = [keep.tile([P, T], U32, name="tab2_win0", align_bytes=64), keep.tile([P, T], U32, name="tab2_win1", align_bytes=64)]
        tab_win = [keep.tile([P, T], U32, name="tab_win0", tag="H", align_bytes=64), keep.tile([P, T], U32, name="tab_win1", tag="I", align_bytes=64), keep.tile([P, T], U32, name="tab_win2", align_bytes=64)]
        w1_raw = [keep.tile([P, 4, H], F32, name="w1_raw0", tag="C", align_bytes=64), keep.tile([P, 4, H], F32, name="w1_raw1", align_bytes=64), keep.tile([P, 4, H], F32, name="w1_raw2", align_bytes=64)]
        wb_raw = keep.tile([P, 2, H], U32, name="wb_raw", align_bytes=64)
        ws_raw = keep.tile([P, 2 * H], U8, name="ws_raw", align_bytes=64)
        wo_raw = keep.tile([P, 4, N], F32, name="wo_raw", tag="C", align_bytes=64)
        wg = keep.tile([P, 4, PS], F32, name="wg")
        wgs_sb = keep.tile([P, PS], F32, name="wgs_sb")
        turn_sb = keep.tile([P, 4], F32, name="turn_sb")
        swing_sb = keep.tile([P, 4], F32, name="swing_sb")
        grip_sb = keep.tile([P, 4], F32, name="grip_sb")
        w1_rows = w1.rearrange("(a p j) c -> a p j c", a=3, j=4)

        def load_scale_rows(queue, plane, scales):
            rows = 4 * scales.shape[0]
            for q in range(4):
                queue.dma_start(plane[32 * q : 32 * q + rows, :].bitcast(I32), scales[:, 4 * q : 4 * q + 4, :].bitcast(I32))


        nc.sync.dma_start(idx[:], offs)
        nc.sync.dma_start(tab_win[0][:].bitcast(I32), words_view(tab_words, 0))
        load_scale_rows(nc.scalar, tab_sc, tab_scales)
        nc.sync.dma_start(wgs_sb[:], wgs)
        nc.scalar.dma_start(grip_sb[:], grip.rearrange("(p t) -> p t", t=4))
        nc.scalar.dma_start(turn_sb[:], turn.rearrange("(p t) -> p t", t=4))
        nc.scalar.dma_start(swing_sb[:], swing.rearrange("(p t) -> p t", t=4))
        load_scale_rows(nc.gpsimd, tab2_sc, tab2_scales)
        load_scale_rows(nc.gpsimd, wbsc_raw, wb_scales)
        nc.sync.dma_start(w1_raw[0][:], w1_rows[0])
        nc.sync.dma_start(idx2[:], offs2)
        nc.sync.dma_start(tab_win[1][:].bitcast(I32), words_view(tab_words, 1))
        nc.sync.dma_start(w1_raw[1][:], w1_rows[1])
        nc.sync.dma_start(ws_raw[:].bitcast(I32), ws_words[0].bitcast(I32))
        load_scale_rows(nc.sync, wssc_raw, ws_scales)
        nc.sync.dma_start(w1_raw[2][:], w1_rows[2])
        nc.sync.dma_start(tab_win[2][:].bitcast(I32), words_view(tab_words, 2))
        nc.sync.dma_start(tab2_win[0][:].bitcast(I32), words_view(tab2_words, 0))
        nc.sync.dma_start(wb_raw[:].bitcast(I32), wb_words.rearrange("a p e i -> p a (e i)").bitcast(I32))
        nc.sync.dma_start(tab2_win[1][:].bitcast(I32), words_view(tab2_words, 1))
        nc.sync.dma_start(place[:], pos1)
        nc.sync.dma_start(wo_raw[:], wo.rearrange("(p j) n -> p j n", j=4))

        turned = psum.tile([P, 4, P], F32, name="bank")
        for b in range(4):
            nc.tensor.transpose(turned[:, b, :], wgs_sb[:, P * b : P * (b + 1)], ident[:])
        spread = []
        dealt = keep.tile([P, 4, 4, P], F32, name="dealt", tag="F", align_bytes=64)
        for t in range(4):
            nc.scalar.copy(
                dealt[:, t, :, :].rearrange("p b (r q) -> p b r q", r=4),
                turned[:].rearrange("p b (q t) -> p b t q", t=4)[:, :, t : t + 1, :].to_broadcast([P, 4, 4, 32]),
            )
            bank = psum.tile([P, 4, P], F32, name="bank")
            for b in range(4):
                nc.tensor.transpose(bank[:, b, :], dealt[:, t, b, :], ident[:])
            spread.append(bank)

        v2_sc = keep.tile([P, PS], U8, name="v2_sc", align_bytes=64)
        v_sc = keep.tile([P, S], U8, name="v_sc", align_bytes=64)
        v2 = [keep.tile([P, PS], U32, name=f"survey{a}", align_bytes=64) for a in range(2)]
        for a in range(2):
            nc.vector.tensor_copy(v2[a][:], tab2_win[a][:].indirect(idx2[:]))
        nc.vector.tensor_copy(v2_sc[:], tab2_sc[:].indirect(idx2[:]))

        wb_q = keep.tile([P, 2, H], U32, name="wb_q", align_bytes=64)
        wb_sc = keep.tile([P, H], U8, name="wb_sc", align_bytes=64)
        nc.vector.tensor_copy(
            wb_q[:].bitcast(I32).rearrange("p a (t q) -> p a q t", t=4),
            wb_raw[:].bitcast(I32).rearrange("p a (q t) -> p a q t", t=4),
        )
        nc.gpsimd.tensor_copy(wb_sc[:].rearrange("p (t q) -> p q t", t=4), wbsc_raw[:].rearrange("p (q t) -> p q t", t=4))

        def scatter(t, factor):
            for u in range(1):
                n = PS // 1
                nc.vector.tensor_tensor(
                    placed[t][:].indirect(place[:, n // 16 * u : n // 16 * (u + 1)]),
                    th[t][:, n * u : n * (u + 1)], factor[:, n * u : n * (u + 1)], ALU.mult,
                )


        v = [[keep.tile([P, HALF], U32, name=f"v{a}_{h}", align_bytes=64) for h in range(2)] for a in range(3)]
        w1_q = [keep.tile([P, H], U32, name=f"w1_q{a}", align_bytes=64) for a in range(3)]
        w1_sc = [keep.tile([P, H], U8, name=f"w1_sc{a}", align_bytes=64) for a in range(3)]
        nc.vector.tensor_copy(v_sc[:], tab_sc[:].indirect(idx[:]))
        w1_bfs = [keep.tile([P, 4 * H], BF16, name=f"w1_bf{a}", align_bytes=64) for a in range(3)]
        for a in range(3):
            w1_bf = w1_bfs[a]
            nc.scalar.copy(
                w1_bf[:].rearrange("p (t m j) -> p m j t", t=4, j=4),
                w1_raw[a][:].rearrange("p j (m t) -> p m j t", t=4),
            )
            nc.vector.quantize_mx(out=w1_q[a][:].bitcast(FP8X4), scales=w1_sc[a][:], in_=w1_bf[:])
            for h in range(2):
                nc.vector.tensor_copy(v[a][h][:], tab_win[a][:].indirect(idx[:, 32 * h : 32 * (h + 1)]))

        for t in range(4):
            nc.scalar.activation(
                out=wg[:, t, :], in_=spread[t][:].rearrange("p b j -> p (b j)"), func=ACT.Copy, scale=grip_sb[:, t : t + 1]
            )
        turns = keep.tile([P, 4], F32, name="turns")
        nc.vector.tensor_scalar(turns[:], turn_sb[:], 1.0 / TWO_PI, 0.0, ALU.mult, ALU.add)

        c_sb = [keep.tile([P, 4, HALF], F32, name="c_sb0", align_bytes=64), keep.tile([P, 4, HALF], F32, name="c_sb1", tag="H", align_bytes=64)]
        x_q = [keep.tile([P, HALF], U32, name=f"x_q{h}", align_bytes=64) for h in range(2)]
        x_sc = [keep.tile([P, HALF], U8, name=f"x_sc{h}", align_bytes=64) for h in range(2)]

        wholes = [keep.tile([P, HALF], I32, name=f"whole{i}") for i in range(4)]
        x_bfs = [keep.tile([P, 4 * HALF], BF16, name=f"x_bf{h}", align_bytes=64) for h in range(2)]

        fracs = [keep.tile([P, 4, HALF], F32, name="frac0", tag="F", align_bytes=64), keep.tile([P, 4, HALF], F32, name="frac1", tag="I", align_bytes=64)]

        late = keep.tile([P, 4 * S + 0], F32, name="late", align_bytes=64)
        joined = late[:, 0 : 4 * S].rearrange("p (t j) -> p t j", t=4)
        x_room0 = keep.tile([P, HALF + 2 * N], F32, name="x_room0", align_bytes=64)
        wo_bf = x_room0[:, HALF : HALF + 2 * N].bitcast(BF16)
        x_rooms = [x_room0[:, 0 : 2 * HALF].bitcast(BF16), late[:, 3 * S : 4 * S].bitcast(BF16)]

        def load_features(h):
            frac = fracs[h]
            for t in range(4):
                cols = slice(P * t, P * (t + 1))
                bank = psum.tile([P, HALF], F32, name="bank")
                for a in range(3):
                    nc.tensor.matmul_mx(
                        out=bank[:], lhsT=w1_q[a][:, cols].bitcast(FP8X4), lhsT_scale=w1_sc[a][:, cols],
                        rhs=v[a][h][:].bitcast(FP8X4), rhs_scale=v_sc[4 * a : P, HALF * h : HALF * (h + 1)],
                        start=(a == 0), stop=(a == 2),
                    )
                nc.scalar.copy(c_sb[h][:, t, :], bank[:])
                whole = wholes[(4 * h + t) % len(wholes)]
                nc.gpsimd.tensor_scalar(whole[:], c_sb[h][:, t, :], turns[:, t : t + 1], 0.0, ALU.mult, ALU.add)
                nc.vector.scalar_tensor_tensor(
                    frac[:, t, :], bank[:], turns[:, t : t + 1], whole[:], ALU.mult, ALU.subtract
                )

        def swing_features(h, on_vector):
            frac = fracs[h]
            x_bf = x_bfs[h]
            x_rows = x_rooms[h].rearrange("p (t j) -> p t j", t=4)
            for t in range(4):
                nc.scalar.activation(out=frac[:, t, :], in_=frac[:, t, :], func=ACT.Sin, scale=TWO_PI)
                if not on_vector:
                    nc.scalar.activation(out=x_rows[:, t, :], in_=frac[:, t, :], func=ACT.Copy, scale=swing_sb[:, t : t + 1])
            woven = x_bf[:].rearrange("p (c i t) -> p c t i", i=4, t=4)
            if on_vector:
                nc.vector.tensor_tensor(
                    woven, frac[:].rearrange("p t (c i) -> p c t i", i=4),
                    swing_sb[:].unsqueeze(1).unsqueeze(3).to_broadcast([P, HALF // 4, 4, 4]), ALU.mult,
                )
            else:
                nc.scalar.copy(woven, x_rows[:].rearrange("p t (c i) -> p c t i", i=4))
            nc.vector.quantize_mx(out=x_q[h][:].bitcast(FP8X4), scales=x_sc[h][:], in_=x_bf[:])

        load_features(0)
        load_features(1)
        survey = []
        th = [None] * 4
        for t in range(4):
            cols = slice(P * t, P * (t + 1))
            bank = psum.tile([P, HALF], F32, name="bank")
            for a in range(2):
                nc.tensor.matmul_mx(
                    out=bank[:], lhsT=wb_q[:, a, cols].bitcast(FP8X4), lhsT_scale=wb_sc[4 * a : P, cols],
                    rhs=v2[a][:].bitcast(FP8X4), rhs_scale=v2_sc[4 * a : P, :], start=(a == 0), stop=(a == 1),
                )
            survey.append(bank)
        th[0] = keep.tile([P, HALF], F32, name="th0")
        nc.scalar.activation(out=th[0][:], in_=survey[0][:], func=ACT.Tanh)
        th[1] = keep.tile([P, HALF], F32, name="th1")
        nc.scalar.activation(out=th[1][:], in_=survey[1][:], func=ACT.Tanh)

        swing_features(0, False)
        th[2] = x_room0[:, 0:HALF]
        nc.scalar.activation(out=th[2][:], in_=survey[2][:], func=ACT.Tanh)
        ws_q = keep.tile([P, 2 * H], U8, name="ws_q", align_bytes=64)
        ws_sc = keep.tile([P, H], U8, name="ws_sc", align_bytes=64)
        nc.vector.tensor_copy(
            ws_q[:].rearrange("p (t q b) -> p q t b", t=4, b=2), ws_raw[:].rearrange("p (q t b) -> p q t b", t=4, b=2)
        )
        nc.vector.tensor_copy(ws_sc[:].rearrange("p (t q) -> p q t", t=4), wssc_raw[:].rearrange("p (q t) -> p q t", t=4))
        wo_q = keep.tile([P, N], U32, name="wo_q", align_bytes=64)
        wo_sc = keep.tile([P, N], U8, name="wo_sc", align_bytes=64)
        nc.scalar.copy(
            wo_bf[:].rearrange("p (c i j) -> p c j i", i=4, j=4), wo_raw[:].rearrange("p j (c i) -> p c j i", i=4)
        )
        for lo, hi in ((0, 512), (512, N)):
            nc.vector.quantize_mx(out=wo_q[:, lo:hi].bitcast(FP8X4), scales=wo_sc[:, lo:hi], in_=wo_bf[:, 4 * lo : 4 * hi])

        swing_features(1, False)


        th[3] = fracs[1][:, 1, :]
        nc.scalar.activation(out=th[3][:], in_=survey[3][:], func=ACT.Tanh)
        for t in range(4):
            scatter(t, wg[:, t, :])
        for t in range(3):
            nc.sync.dma_start(joined[:, t, :], placed[t][:])
        for h in range(2):
            nc.scalar.copy(joined[:, 3, HALF * h : HALF * (h + 1)], placed[3][:, HALF * h : HALF * (h + 1)])
        flat = "p a b -> p (a b)"
        rooms = [w1_raw[1][:].rearrange(flat), w1_raw[2][:].rearrange(flat), wo_raw[:].rearrange(flat)]
        stages = [rooms[0], rooms[0][:, 640:2048], rooms[1]] + [rooms[2][:, 640 * i : 2560] for i in range(4)]
        swung = [[], []]
        for h in range(2):
            for u in range(4):
                bank = psum.tile([P, 4, P], F32, name="bank")
                for t in range(4):
                    nc.tensor.matmul_mx(
                        out=bank[:, t, :], lhsT=ws_q[:, 2 * P * t : 2 * P * (t + 1)].bitcast(FP4X4), lhsT_scale=ws_sc[:, P * t : P * (t + 1)],
                        rhs=x_q[h][:, P * u : P * (u + 1)].bitcast(FP8X4), rhs_scale=x_sc[h][:, P * u : P * (u + 1)], start=True, stop=True,
                    )
                swung[h].append(bank)
        out_rows = out.rearrange("(n p) j -> p n j", p=P)
        for h, pieces in enumerate(((128, 128, 256,), (128, 128, 128, 128,))):
            larger = fracs[h]
            z_bf = w1_bfs[h]
            z_q = ring.tile([P, HALF], U32, name="z_q", align_bytes=64)
            z_sc = ring.tile([P, HALF], U8, name="z_sc", align_bytes=64)
            lo = 0
            for width in pieces:
                js = slice(lo, lo + width)
                for u in range(lo // P, (lo + width) // P):
                    us = slice(P * u, P * (u + 1))
                    nc.vector.tensor_tensor(larger[:, :, us], swung[h][u][:], c_sb[h][:, :, us], ALU.max)
                z_piece = z_bf[:, 4 * lo : 4 * (lo + width)]
                nc.vector.tensor_tensor(
                    z_piece.rearrange("p (c i t) -> p c t i", i=4, t=4),
                    larger[:, :, js].rearrange("p t (c i) -> p c t i", i=4),
                    joined[:, :, HALF * h + lo : HALF * h + lo + width].rearrange("p t (c i) -> p c t i", i=4),
                    ALU.add,
                )
                nc.vector.quantize_mx(out=z_q[:, js].bitcast(FP8X4), scales=z_sc[:, js], in_=z_piece)
                stage = stages.pop(0)[:, 0 : 5 * width].rearrange("p (n j) -> p n j", n=5)
                per_bank = HALF // width
                for b, n0 in enumerate(range(0, 5, per_bank)):
                    ns = list(range(n0, min(n0 + per_bank, 5)))
                    bank = psum.tile([P, HALF], F32, name="bank")
                    for i, n in enumerate(ns):
                        cols = slice(P * n, P * (n + 1))
                        nc.tensor.matmul_mx(
                            out=bank[:, width * i : width * (i + 1)], lhsT=wo_q[:, cols].bitcast(FP8X4), lhsT_scale=wo_sc[:, cols],
                            rhs=z_q[:, js].bitcast(FP8X4), rhs_scale=z_sc[:, js], start=True, stop=True,
                        )
                    last = h == 1 and lo + width == HALF
                    copy = nc.vector.tensor_copy if last and b == 0 else nc.scalar.copy
                    copy(stage[:, n0 : n0 + len(ns), :].rearrange("p n j -> p (n j)"), bank[:, 0 : width * len(ns)])
                j0 = HALF * h + lo
                nc.sync.dma_start(out_rows[:, :, j0 : j0 + width], stage[:])
                lo += width
